import numpy as np
import ml_dtypes


def mxq(x, axis, fmt="e4m3"):
    dtype, down = {"e4m3": (ml_dtypes.float8_e4m3fn, 7), "e5m2": (ml_dtypes.float8_e5m2, 14)}[fmt]
    v = np.moveaxis(np.asarray(x, np.float32).astype(ml_dtypes.bfloat16).astype(np.float64), axis, -1)
    blocks = v.reshape(v.shape[:-1] + (-1, 32))
    amax = np.abs(blocks).max(-1, keepdims=True)
    byte = np.maximum(np.where(amax > 0, np.frexp(amax)[1] - 1 + 127, 0) - down, 1)
    scale = np.exp2(byte - 127.0)
    codes = (blocks / scale).astype(np.float32).astype(dtype).astype(np.float64)
    return np.moveaxis((codes * scale).reshape(v.shape), -1, axis)


WIDE = False


def mx_kscale(k):
    if not WIDE:
        return np.ones(k)
    levels = np.array([10, -10, 5, -5, 0])
    if k % 512:
        return np.exp2(np.random.permutation(np.resize(levels, k // 32))).repeat(32)
    a = np.empty((k // 512, 16))
    for p in range(k // 512):
        a[p, :8] = np.random.permutation(np.resize(levels, 8))
        for g in range(8):
            far = levels[np.abs(levels - a[p, g]) >= 10]
            a[p, g + 8] = far[np.random.randint(len(far))]
    return np.exp2(a.ravel()).repeat(32)


def f64(x):
    return np.asarray(x).astype(np.float64)


def striped(idx):
    return np.tile(idx.reshape(-1, 16).T, (8, 1)).astype(np.uint16)


def unstriped(offs):
    return offs[:16].T.reshape(-1).astype(np.int64)


def pack_weight(w):
    k, n = w.shape
    w = f64(np.asarray(w, np.float32).astype(ml_dtypes.bfloat16)).reshape(k // 32, 32, n)
    amax = np.abs(w).max(1)
    byte = np.clip(np.where(amax > 0, np.frexp(amax)[1] - 1 + 127 - 7, 1), 1, 254)
    scaled = (w * np.exp2(127.0 - byte)[:, None, :]).reshape(k, n).astype(np.float32)
    words = np.ascontiguousarray(scaled.reshape(k // 512, 128, 4, n).transpose(0, 1, 3, 2)).astype(ml_dtypes.float8_e4m3fn).view(np.uint8)
    return words, np.ascontiguousarray(byte.astype(np.uint8).reshape(k // 512, 16, n))


def unpack_weight(words, scales):
    g, p, n, _ = words.shape
    vals = np.ascontiguousarray(words).view(ml_dtypes.float8_e4m3fn).astype(np.float64) * np.repeat(np.exp2(scales.astype(np.float64) - 127.0), 8, axis=1)[..., None]
    return vals.transpose(0, 1, 3, 2).reshape(g * 512, n)


def sigmoid(v):
    return 1.0 / (1.0 + np.exp(-np.maximum(v, -700.0)))


K, T, S, N, H, U = 512, 2048, 512, 128, 512, 1024


def setup_inputs():
    n = np.random.standard_normal
    s = mx_kscale(K)[:, None]
    u = mx_kscale(H)
    packed_xT = pack_weight(n((K, T)) * s)
    return {
        "x_words": packed_xT[0],
        "x_scales": packed_xT[1],
        "w1": (n((K, H)) / np.sqrt(K) / s).astype(np.float32),
        "w2": (n((K, H)) / np.sqrt(K) / s).astype(np.float32),
        "g0": (np.random.uniform(0.3, 1.5, (H, U))).astype(np.float32),
        "cap": (np.random.uniform(0.8, 1.6, (H, U))).astype(np.float32),
        "unit": (np.random.uniform(0.6, 1.4, (H, 1)) * u[:, None]).astype(np.float32),
        "w3": (n((H, N)) / np.sqrt(H) / u[:, None]).astype(np.float32),
        "offs": striped(np.random.permutation(T)[:S]),
        "m1": striped(np.random.permutation(np.concatenate([np.arange(S), np.random.randint(0, S, U - S)]))),
        "m2": striped(np.random.permutation(np.concatenate([np.arange(S), np.random.randint(0, S, U - S)]))),
    }


def reference(x_words, x_scales, w1, w2, g0, cap, unit, w3, offs, m1, m2):
    xq = unpack_weight(x_words, x_scales)[:, unstriped(offs)]
    y = mxq(f64(w1), 0, "e4m3").T @ xq
    a1 = y[:, unstriped(m1)]
    a2 = y[:, unstriped(m2)]
    ep = mxq(f64(w2), 0, "e4m3").T @ xq
    e1 = ep[:, unstriped(m1)]
    e2 = ep[:, unstriped(m2)]
    epi = e1 * e2
    ddg = a1 + a2 + 0.7 * epi
    fold = sigmoid(f64(g0) - ddg)
    acr = np.minimum(np.exp(-1.0 * ddg), f64(cap))
    hid = f64(unit) * (fold * acr)
    return mxq(f64(w3), 0, "e4m3").T @ mxq(hid, 0, "e4m3")

@@ -1,0 +1,190 @@
+from contextlib import ExitStack
+
+import concourse.mybir as mybir
+
+K, T, S, N, H, U = 512, 2048, 512, 128, 512, 1024
+FLOPS = 2 * K * H * S * 2 + 2 * H * N * U
+
+F32 = mybir.dt.float32
+BF16 = mybir.dt.bfloat16
+I32 = mybir.dt.int32
+U32 = mybir.dt.uint32
+U16 = mybir.dt.uint16
+U8 = mybir.dt.uint8
+FP8X4 = mybir.dt.float8_e4m3fn_x4
+ALU = mybir.AluOpType
+ACT = mybir.ActivationFunctionType
+
+P = 128
+PACK = 4
+HALF = 512
+HALVES = U // HALF
+SPARE = 16
+EPISTASIS = 0.7
+
+
+def tile_picked_ymetmu_mh_p_kernel(
+    tc, x_words, x_scales, w1, w2, g0, cap, unit, w3, offs, m1, m2, out
+):
+    nc = tc.nc
+    with ExitStack() as ctx:
+        keep = ctx.enter_context(tc.tile_pool(name="keep", bufs=1))
+        ring = ctx.enter_context(tc.tile_pool(name="ring", bufs=3))
+        psum = ctx.enter_context(tc.psum_pool(name="psum", bufs=4))
+
+        def tile(name, shape, dtype):
+            return keep.tile(shape, dtype, name=name, align_bytes=64)
+
+        offs_sb = tile("offs_sb", [P, S // 16], U16)
+        nc.sync.dma_start(offs_sb[:], offs)
+
+        all_scales = tile("all_scales", [P, T], U8)
+        nc.vector.memset(all_scales[:].bitcast(I32), 0)
+        for q in range(4):
+            nc.sync.dma_start(
+                all_scales[32 * q : 32 * q + 4, :].bitcast(I32),
+                x_scales[0, 4 * q : 4 * q + 4, :].bitcast(I32),
+            )
+        all_words = tile("all_words", [P, T], I32)
+        nc.sync.dma_start(all_words[:], x_words[0].rearrange("p c r -> p (c r)").bitcast(I32))
+
+        def load_weight(name, w):
+            parts = []
+            for c in range(2):
+                raw = tile(name + "_raw%d" % c, [P, PACK, H // 2], F32)
+                nc.sync.dma_start(raw[:], w.rearrange("(p j) c -> p j c", j=PACK)[:, :, c * (H // 2) : (c + 1) * (H // 2)])
+                parts.append(raw)
+            return parts
+
+        w2_raw = load_weight("w2", w2)
+        m1_sb = tile("m1_sb", [P, U // 16], U16)
+        nc.sync.dma_start(m1_sb[:], m1)
+        m2_sb = tile("m2_sb", [P, U // 16], U16)
+        nc.sync.dma_start(m2_sb[:], m2)
+        w1_raw = load_weight("w1", w1)
+
+        def load_rows(name, src):
+            tiles = []
+            for t in range(PACK):
+                rows = tile(name + "%d" % t, [P, U], F32)
+                nc.sync.dma_start(rows[:], src.rearrange("(p t) r -> p t r", t=PACK)[:, t, :])
+                tiles.append(rows)
+            return tiles
+
+        g0_sb = load_rows("g0_", g0)
+        w3_raw = tile("w3_raw", [P, PACK, N], F32)
+        nc.sync.dma_start(w3_raw[:], w3.rearrange("(p j) n -> p j n", j=PACK))
+        unit_sb = tile("unit_sb", [P, PACK], F32)
+        nc.sync.dma_start(unit_sb[:], unit.rearrange("(p t) o -> p (t o)", t=PACK))
+        cap_sb = load_rows("cap_", cap)
+
+        x_sc = tile("x_sc", [P, S], U8)
+        nc.vector.tensor_copy(x_sc[:], all_scales[:].indirect(offs_sb[:]))
+        x_wd = tile("x_wd", [P, S], I32)
+        nc.vector.tensor_copy(x_wd[:].bitcast(U32), all_words[:].bitcast(U32).indirect(offs_sb[:]))
+
+        def tables(name, raw_parts, engines):
+            dealt = tile(name + "_dealt", [P, PACK, P, PACK], BF16)
+            for c, raw in enumerate(raw_parts):
+                dst = dealt[:, :, c * (P // 2) : (c + 1) * (P // 2), :].rearrange("p t m j -> p m t j")
+                src = raw[:].rearrange("p j (m t) -> p m t j", t=PACK)
+                if engines[c] == "s":
+                    nc.scalar.copy(dst, src)
+                else:
+                    nc.vector.tensor_copy(dst, src)
+            res = []
+            for t in range(PACK):
+                codes = tile(name + "_codes%d" % t, [P, P], U32)
+                scales = tile(name + "_scales%d" % t, [P, P], U8)
+                nc.vector.quantize_mx(codes[:].bitcast(FP8X4), scales[:], dealt[:, t].rearrange("p m j -> p (m j)"))
+                acc = psum.tile([P, S], F32, name=name + "_acc")
+                nc.tensor.matmul_mx(
+                    acc[:], lhsT=codes[:].bitcast(FP8X4), lhsT_scale=scales[:],
+                    rhs=x_wd[:].bitcast(FP8X4), rhs_scale=x_sc[:], start=True, stop=True,
+                )
+                res.append(acc)
+            return res
+
+        def window(name):
+            win = tile(name, [P, S + SPARE], F32)
+            nc.gpsimd.memset(win[:, S:], 0.0)
+            return win
+
+        ep_win = [window("ep_win%d" % t) for t in range(PACK)]
+        y_win = [window("y_win%d" % t) for t in range(PACK)]
+
+        ep_acc = tables("w2", w2_raw, "sv")
+        y_acc = tables("w1", w1_raw, "vv")
+
+        def picks(lst, h):
+            return lst[:, h * (HALF // 16) : (h + 1) * (HALF // 16)]
+
+        def cols(h):
+            return slice(h * HALF, (h + 1) * HALF)
+
+        ddg, arg, ratio = {}, {}, {}
+        for t in range(PACK):
+            nc.scalar.copy(ep_win[t][:, :S], ep_acc[t][:])
+            e1, epi, a2, part = {}, {}, {}, {}
+            for h in range(HALVES):
+                e1[h] = ring.tile([P, HALF], F32, name="e1")
+                nc.scalar.activation(e1[h][:], ep_win[t][:].indirect(picks(m1_sb, h)), ACT.Copy, scale=EPISTASIS)
+            nc.scalar.copy(y_win[t][:, :S], y_acc[t][:])
+            for h in range(HALVES):
+                epi[h] = ring.tile([P, HALF], F32, name="epi")
+                nc.vector.tensor_tensor(epi[h][:], ep_win[t][:].indirect(picks(m2_sb, h)), e1[h][:], ALU.mult)
+            for h in range(HALVES):
+                a2[h] = ring.tile([P, HALF], F32, name="a2")
+                nc.scalar.activation(a2[h][:], y_win[t][:].indirect(picks(m2_sb, h)), ACT.Copy)
+            for h in range(HALVES):
+                part[h] = ring.tile([P, HALF], F32, name="part")
+                nc.vector.tensor_tensor(part[h][:], y_win[t][:].indirect(picks(m1_sb, h)), epi[h][:], ALU.add)
+            for h in range(HALVES):
+                ddg[t, h] = tile("ddg%d_%d" % (t, h), [P, HALF], F32)
+                nc.vector.tensor_tensor(ddg[t, h][:], part[h][:], a2[h][:], ALU.add)
+            for h in range(HALVES):
+                arg[t, h] = tile("arg%d_%d" % (t, h), [P, HALF], F32)
+                nc.vector.tensor_tensor(arg[t, h][:], g0_sb[t][:, cols(h)], ddg[t, h][:], ALU.subtract)
+                ratio[t, h] = tile("ratio%d_%d" % (t, h), [P, HALF], F32)
+                nc.scalar.activation(ratio[t, h][:], ddg[t, h][:], ACT.Exp, scale=-1.0)
+
+        w3_dealt = tile("w3_dealt", [P, N, PACK], BF16)
+        nc.vector.tensor_copy(w3_dealt[:], w3_raw[:].rearrange("p j n -> p n j"))
+        w3_codes = tile("w3_codes", [P, N], U32)
+        w3_scales = tile("w3_scales", [P, N], U8)
+        nc.vector.quantize_mx(w3_codes[:].bitcast(FP8X4), w3_scales[:], w3_dealt[:].rearrange("p n j -> p (n j)"))
+
+        order = [(t, h) for h in range(HALVES) for t in range(PACK)]
+        acr = {}
+        for t, h in order:
+            acr[t, h] = tile("acr%d_%d" % (t, h), [P, HALF], F32)
+            nc.vector.tensor_tensor(acr[t, h][:], ratio[t, h][:], cap_sb[t][:, cols(h)], ALU.min)
+
+        spent = ddg[PACK - 1, HALVES - 1]
+        for h in range(HALVES):
+            hid = tile("hid%d" % h, [P, PACK, HALF], BF16)
+            for t in range(PACK):
+                fold = spent
+                nc.scalar.activation(fold[:], arg[t, h][:], ACT.Sigmoid)
+                spent = arg[t, h]
+                nc.vector.scalar_tensor_tensor(
+                    hid[:, t, :], fold[:], unit_sb[:, t : t + 1], acr[t, h][:], ALU.mult, ALU.mult
+                )
+            woven = tile("woven%d" % h, [P, HALF, PACK], BF16)
+            dst = woven[:].rearrange("p (c i) t -> p c t i", i=4)
+            src = hid[:].rearrange("p t (c i) -> p c t i", i=4)
+            if h == 0:
+                nc.scalar.copy(dst, src)
+            else:
+                nc.vector.tensor_copy(dst, src)
+            hid_codes = tile("hid_codes%d" % h, [P, HALF], U32)
+            hid_scales = tile("hid_scales%d" % h, [P, HALF], U8)
+            nc.vector.quantize_mx(hid_codes[:].bitcast(FP8X4), hid_scales[:], woven[:].rearrange("p c t -> p (c t)"))
+            acc = psum.tile([P, HALF], F32, name="w2_acc")
+            nc.tensor.matmul_mx(
+                acc[:], lhsT=w3_codes[:].bitcast(FP8X4), lhsT_scale=w3_scales[:],
+                rhs=hid_codes[:].bitcast(FP8X4), rhs_scale=hid_scales[:], start=True, stop=True,
+            )
+            res = tile("res%d" % h, [P, HALF], F32)
+            nc.scalar.copy(res[:], acc[:])
+            nc.sync.dma_start(out[:, cols(h)], res[:])

@@ -1,6 +1,7 @@
 from contextlib import ExitStack
 
 import concourse.mybir as mybir
+from concourse.masks import make_identity
 
 K, T, S, N, H, U = 512, 2048, 512, 128, 512, 1024
 FLOPS = 2 * K * H * S * 2 + 2 * H * N * U
@@ -29,24 +30,19 @@ def tile_picked_ymetmu_mh_p_kernel(
     nc = tc.nc
     with ExitStack() as ctx:
         keep = ctx.enter_context(tc.tile_pool(name="keep", bufs=1))
-        ring = ctx.enter_context(tc.tile_pool(name="ring", bufs=3))
-        psum = ctx.enter_context(tc.psum_pool(name="psum", bufs=4))
+        ring = ctx.enter_context(tc.tile_pool(name="ring", bufs=5))
+        psum = ctx.enter_context(tc.psum_pool(name="psum", bufs=1))
 
         def tile(name, shape, dtype):
             return keep.tile(shape, dtype, name=name, align_bytes=64)
 
-        offs_sb = tile("offs_sb", [P, S // 16], U16)
-        nc.sync.dma_start(offs_sb[:], offs)
+        def bank(b):
+            return psum.tile([P, HALF], F32, name="bank%d" % b)
 
-        all_scales = tile("all_scales", [P, T], U8)
-        nc.vector.memset(all_scales[:].bitcast(I32), 0)
-        for q in range(4):
-            nc.sync.dma_start(
-                all_scales[32 * q : 32 * q + 4, :].bitcast(I32),
-                x_scales[0, 4 * q : 4 * q + 4, :].bitcast(I32),
-            )
-        all_words = tile("all_words", [P, T], I32)
-        nc.sync.dma_start(all_words[:], x_words[0].rearrange("p c r -> p (c r)").bitcast(I32))
+        def load_list(name, src):
+            lst = tile(name, src.shape, U16)
+            nc.sync.dma_start(lst[:], src)
+            return lst
 
         def load_weight(name, w):
             parts = []
@@ -56,13 +52,6 @@ def tile_picked_ymetmu_mh_p_kernel(
                 parts.append(raw)
             return parts
 
-        w2_raw = load_weight("w2", w2)
-        m1_sb = tile("m1_sb", [P, U // 16], U16)
-        nc.sync.dma_start(m1_sb[:], m1)
-        m2_sb = tile("m2_sb", [P, U // 16], U16)
-        nc.sync.dma_start(m2_sb[:], m2)
-        w1_raw = load_weight("w1", w1)
-
         def load_rows(name, src):
             tiles = []
             for t in range(PACK):
@@ -71,6 +60,21 @@ def tile_picked_ymetmu_mh_p_kernel(
                 tiles.append(rows)
             return tiles
 
+        all_scales = tile("all_scales", [P, T], U8)
+        nc.vector.memset(all_scales[:].bitcast(I32), 0)
+
+        offs_sb = load_list("offs_sb", offs)
+        for q in range(4):
+            nc.sync.dma_start(
+                all_scales[32 * q : 32 * q + 4, :].bitcast(I32),
+                x_scales[0, 4 * q : 4 * q + 4, :].bitcast(I32),
+            )
+        all_words = tile("all_words", [P, T], I32)
+        nc.sync.dma_start(all_words[:], x_words[0].rearrange("p c r -> p (c r)").bitcast(I32))
+        w2_raw = load_weight("w2", w2)
+        m1_sb = load_list("m1_sb", m1)
+        m2_sb = load_list("m2_sb", m2)
+        w1_raw = load_weight("w1", w1)
         g0_sb = load_rows("g0_", g0)
         w3_raw = tile("w3_raw", [P, PACK, N], F32)
         nc.sync.dma_start(w3_raw[:], w3.rearrange("(p j) n -> p j n", j=PACK))
@@ -78,32 +82,8 @@ def tile_picked_ymetmu_mh_p_kernel(
         nc.sync.dma_start(unit_sb[:], unit.rearrange("(p t) o -> p (t o)", t=PACK))
         cap_sb = load_rows("cap_", cap)
 
-        x_sc = tile("x_sc", [P, S], U8)
-        nc.vector.tensor_copy(x_sc[:], all_scales[:].indirect(offs_sb[:]))
-        x_wd = tile("x_wd", [P, S], I32)
-        nc.vector.tensor_copy(x_wd[:].bitcast(U32), all_words[:].bitcast(U32).indirect(offs_sb[:]))
-
-        def tables(name, raw_parts, engines):
-            dealt = tile(name + "_dealt", [P, PACK, P, PACK], BF16)
-            for c, raw in enumerate(raw_parts):
-                dst = dealt[:, :, c * (P // 2) : (c + 1) * (P // 2), :].rearrange("p t m j -> p m t j")
-                src = raw[:].rearrange("p j (m t) -> p m t j", t=PACK)
-                if engines[c] == "s":
-                    nc.scalar.copy(dst, src)
-                else:
-                    nc.vector.tensor_copy(dst, src)
-            res = []
-            for t in range(PACK):
-                codes = tile(name + "_codes%d" % t, [P, P], U32)
-                scales = tile(name + "_scales%d" % t, [P, P], U8)
-                nc.vector.quantize_mx(codes[:].bitcast(FP8X4), scales[:], dealt[:, t].rearrange("p m j -> p (m j)"))
-                acc = psum.tile([P, S], F32, name=name + "_acc")
-                nc.tensor.matmul_mx(
-                    acc[:], lhsT=codes[:].bitcast(FP8X4), lhsT_scale=scales[:],
-                    rhs=x_wd[:].bitcast(FP8X4), rhs_scale=x_sc[:], start=True, stop=True,
-                )
-                res.append(acc)
-            return res
+        ident = tile("ident", [P, P], F32)
+        make_identity(nc, ident[:])
 
         def window(name):
             win = tile(name, [P, S + SPARE], F32)
@@ -113,8 +93,46 @@ def tile_picked_ymetmu_mh_p_kernel(
         ep_win = [window("ep_win%d" % t) for t in range(PACK)]
         y_win = [window("y_win%d" % t) for t in range(PACK)]
 
-        ep_acc = tables("w2", w2_raw, "sv")
-        y_acc = tables("w1", w1_raw, "vv")
+        def deal(name, raw_parts, copies):
+            dealt = tile(name + "_dealt", [P, PACK, P, PACK], BF16)
+            for c, raw in enumerate(raw_parts):
+                copies[c](
+                    dealt[:, :, c * (P // 2) : (c + 1) * (P // 2), :].rearrange("p t m j -> p m t j"),
+                    raw[:].rearrange("p j (m t) -> p m t j", t=PACK),
+                )
+            return dealt
+
+        def quantize(name, values, width):
+            codes = tile(name + "_codes", [P, width], U32)
+            scales = tile(name + "_scales", [P, width], U8)
+            nc.vector.quantize_mx(codes[:].bitcast(FP8X4), scales[:], values)
+            return codes, scales
+
+        def stationary(name, dealt, groups):
+            res = []
+            for t0, t1 in groups:
+                codes, scales = quantize(name + "_%d" % t0, dealt[:, t0:t1].rearrange("p t m j -> p (t m j)"), (t1 - t0) * P)
+                res.extend((codes[:, k * P : (k + 1) * P], scales[:, k * P : (k + 1) * P]) for k in range(t1 - t0))
+            return res
+
+        x_sc = tile("x_sc", [P, S], U8)
+        nc.vector.tensor_copy(x_sc[:], all_scales[:].indirect(offs_sb[:]))
+        x_wd = tile("x_wd", [P, S], I32)
+        nc.vector.tensor_copy(x_wd[:].bitcast(U32), all_words[:].bitcast(U32).indirect(offs_sb[:]))
+
+        def table(weights, b):
+            codes, scales = weights
+            acc = bank(b)
+            nc.tensor.matmul_mx(
+                acc[:], lhsT=codes.bitcast(FP8X4), lhsT_scale=scales,
+                rhs=x_wd[:].bitcast(FP8X4), rhs_scale=x_sc[:], start=True, stop=True,
+            )
+            return acc
+
+        w2_dealt = deal("w2", w2_raw, (nc.scalar.copy, nc.vector.tensor_copy))
+        ep_acc = [table(w, 2 * t) for t, w in enumerate(stationary("w2", w2_dealt, ((0, 1), (1, 4))))]
+        w1_dealt = deal("w1", w1_raw, (nc.vector.tensor_copy, nc.vector.tensor_copy))
+        y_acc = [table(w, 2 * t + 1) for t, w in enumerate(stationary("w1", w1_dealt, ((0, 1), (1, 4))))]
 
         def picks(lst, h):
             return lst[:, h * (HALF // 16) : (h + 1) * (HALF // 16)]
@@ -122,69 +140,108 @@ def tile_picked_ymetmu_mh_p_kernel(
         def cols(h):
             return slice(h * HALF, (h + 1) * HALF)
 
-        ddg, arg, ratio = {}, {}, {}
-        for t in range(PACK):
-            nc.scalar.copy(ep_win[t][:, :S], ep_acc[t][:])
-            e1, epi, a2, part = {}, {}, {}, {}
+        def turned_sum(acc, terms):
+            for b in range(HALF // P):
+                blk = slice(b * P, (b + 1) * P)
+                for k, term in enumerate(terms):
+                    nc.tensor.matmul(
+                        acc[:, blk], term[:, blk], ident[:], start=(k == 0), stop=(k == len(terms) - 1), is_transpose=True
+                    )
+
+        e1, epi, a2, part, nd, ratio, arg = {}, {}, {}, {}, {}, {}, {}
+        fused = ()
+
+        def first_factors(t):
+            (nc.vector.tensor_copy if t in (2,) else nc.scalar.copy)(ep_win[t][:, :S], ep_acc[t][:])
             for h in range(HALVES):
-                e1[h] = ring.tile([P, HALF], F32, name="e1")
-                nc.scalar.activation(e1[h][:], ep_win[t][:].indirect(picks(m1_sb, h)), ACT.Copy, scale=EPISTASIS)
-            nc.scalar.copy(y_win[t][:, :S], y_acc[t][:])
+                e1[t, h] = ring.tile([P, HALF], F32, name="e1")
+                nc.scalar.activation(e1[t, h][:], ep_win[t][:].indirect(picks(m1_sb, h)), ACT.Copy, scale=-EPISTASIS)
+
+        def products(t):
+            if t in ():
+                nc.vector.tensor_scalar(y_win[t][:, :S], y_acc[t][:], -1.0, None, ALU.mult)
+            else:
+                nc.scalar.activation(y_win[t][:, :S], y_acc[t][:], ACT.Copy, scale=-1.0)
             for h in range(HALVES):
-                epi[h] = ring.tile([P, HALF], F32, name="epi")
-                nc.vector.tensor_tensor(epi[h][:], ep_win[t][:].indirect(picks(m2_sb, h)), e1[h][:], ALU.mult)
+                epi[t, h] = ring.tile([P, HALF], F32, name="epi")
+                nc.vector.tensor_tensor(epi[t, h][:], ep_win[t][:].indirect(picks(m2_sb, h)), e1[t, h][:], ALU.mult)
+
+        def sums(t):
             for h in range(HALVES):
-                a2[h] = ring.tile([P, HALF], F32, name="a2")
-                nc.scalar.activation(a2[h][:], y_win[t][:].indirect(picks(m2_sb, h)), ACT.Copy)
+                if (t, h) not in fused:
+                    a2[t, h] = ring.tile([P, HALF], F32, name="a2")
+                    nc.scalar.activation(a2[t, h][:], y_win[t][:].indirect(picks(m2_sb, h)), ACT.Copy)
             for h in range(HALVES):
-                part[h] = ring.tile([P, HALF], F32, name="part")
-                nc.vector.tensor_tensor(part[h][:], y_win[t][:].indirect(picks(m1_sb, h)), epi[h][:], ALU.add)
+                part[t, h] = ring.tile([P, HALF], F32, name="part")
+                nc.vector.tensor_tensor(part[t, h][:], y_win[t][:].indirect(picks(m1_sb, h)), epi[t, h][:], ALU.add)
             for h in range(HALVES):
-                ddg[t, h] = tile("ddg%d_%d" % (t, h), [P, HALF], F32)
-                nc.vector.tensor_tensor(ddg[t, h][:], part[h][:], a2[h][:], ALU.add)
+                nd[t, h] = tile("nd%d_%d" % (t, h), [P, HALF], F32)
+                if (t, h) in fused:
+                    nc.vector.tensor_tensor(nd[t, h][:], y_win[t][:].indirect(picks(m2_sb, h)), part[t, h][:], ALU.add)
+                else:
+                    nc.vector.tensor_tensor(nd[t, h][:], part[t, h][:], a2[t, h][:], ALU.add)
+
+        def ratios(t):
             for h in range(HALVES):
-                arg[t, h] = tile("arg%d_%d" % (t, h), [P, HALF], F32)
-                nc.vector.tensor_tensor(arg[t, h][:], g0_sb[t][:, cols(h)], ddg[t, h][:], ALU.subtract)
                 ratio[t, h] = tile("ratio%d_%d" % (t, h), [P, HALF], F32)
-                nc.scalar.activation(ratio[t, h][:], ddg[t, h][:], ACT.Exp, scale=-1.0)
+                nc.scalar.activation(ratio[t, h][:], nd[t, h][:], ACT.Exp)
+                arg[t, h] = bank(2 * t + h)
+                turned_sum(arg[t, h], [g0_sb[t][:, cols(h)], nd[t, h][:]])
+
+        first_factors(0)
+        for t in range(PACK):
+            products(t)
+            if t + 1 < PACK:
+                first_factors(t + 1)
+            if t > 0:
+                ratios(t - 1)
+            sums(t)
+        ratios(PACK - 1)
 
         w3_dealt = tile("w3_dealt", [P, N, PACK], BF16)
         nc.vector.tensor_copy(w3_dealt[:], w3_raw[:].rearrange("p j n -> p n j"))
-        w3_codes = tile("w3_codes", [P, N], U32)
-        w3_scales = tile("w3_scales", [P, N], U8)
-        nc.vector.quantize_mx(w3_codes[:].bitcast(FP8X4), w3_scales[:], w3_dealt[:].rearrange("p n j -> p (n j)"))
+        w3_codes, w3_scales = quantize("w3", w3_dealt[:].rearrange("p n j -> p (n j)"), N)
 
-        order = [(t, h) for h in range(HALVES) for t in range(PACK)]
+        last = (PACK - 1, HALVES - 1)
         acr = {}
-        for t, h in order:
-            acr[t, h] = tile("acr%d_%d" % (t, h), [P, HALF], F32)
+        room = [tile("acr%d" % k, [P, HALF], F32) for k in range(0)] + [epi[last], epi[PACK - 1, 0]]
+        for u, (t, h) in enumerate((t, h) for t in range(PACK) for h in range(HALVES)):
+            acr[t, h] = room[u]
+            if u >= 0:
+                room.append(ratio[t, h])
             nc.vector.tensor_tensor(acr[t, h][:], ratio[t, h][:], cap_sb[t][:, cols(h)], ALU.min)
 
-        spent = ddg[PACK - 1, HALVES - 1]
-        for h in range(HALVES):
-            hid = tile("hid%d" % h, [P, PACK, HALF], BF16)
-            for t in range(PACK):
-                fold = spent
-                nc.scalar.activation(fold[:], arg[t, h][:], ACT.Sigmoid)
-                spent = arg[t, h]
-                nc.vector.scalar_tensor_tensor(
-                    hid[:, t, :], fold[:], unit_sb[:, t : t + 1], acr[t, h][:], ALU.mult, ALU.mult
+        spent = [a2[last], part[last], nd[last]]
+        hid = [tile("hid%d" % h, [P, PACK, HALF], BF16) for h in range(HALVES)]
+        for u, (t, h) in enumerate((t, h) for h in range(HALVES) for t in range(PACK)):
+            turned = spent[u % len(spent)]
+            nc.scalar.activation(turned[:], arg[t, h][:], ACT.Sigmoid)
+            fold = bank(2 * t + h)
+            turned_sum(fold, [turned[:]])
+            nc.vector.scalar_tensor_tensor(
+                hid[h][:, t, :], fold[:], unit_sb[:, t : t + 1], acr[t, h][:], ALU.mult, ALU.mult
+            )
+
+        def gpsimd_copy(dst, src):
+            nc.gpsimd.tensor_scalar(dst, src, 1.0, 0.0, ALU.mult, ALU.add)
+
+        engines = {"s": nc.scalar.copy, "v": nc.vector.tensor_copy, "g": gpsimd_copy}
+        pieces = [(0, 0, 256, (("s", 256),), "s"), (0, 256, 256, (("s", 256),), "s"), (1, 0, 256, (("v", 256),), "v"), (1, 256, 256, (("s", 256),), "s")]
+        for n, (h, c0, width, shares, emptier) in enumerate(pieces):
+            woven = tile("woven%d" % n, [P, width, PACK], BF16)
+            at = 0
+            for engine, share in shares:
+                engines[engine](
+                    woven[:, at : at + share, :].rearrange("p (c i) t -> p c t i", i=4),
+                    hid[h][:, :, c0 + at : c0 + at + share].rearrange("p t (c i) -> p c t i", i=4),
                 )
-            woven = tile("woven%d" % h, [P, HALF, PACK], BF16)
-            dst = woven[:].rearrange("p (c i) t -> p c t i", i=4)
-            src = hid[:].rearrange("p t (c i) -> p c t i", i=4)
-            if h == 0:
-                nc.scalar.copy(dst, src)
-            else:
-                nc.vector.tensor_copy(dst, src)
-            hid_codes = tile("hid_codes%d" % h, [P, HALF], U32)
-            hid_scales = tile("hid_scales%d" % h, [P, HALF], U8)
-            nc.vector.quantize_mx(hid_codes[:].bitcast(FP8X4), hid_scales[:], woven[:].rearrange("p c t -> p (c t)"))
-            acc = psum.tile([P, HALF], F32, name="w2_acc")
+                at = at + share
+            hid_codes, hid_scales = quantize("hid%d" % n, woven[:].rearrange("p c t -> p (c t)"), width)
+            acc = bank((0, 2, 4, 6, 1)[n])
             nc.tensor.matmul_mx(
-                acc[:], lhsT=w3_codes[:].bitcast(FP8X4), lhsT_scale=w3_scales[:],
+                acc[:, :width], lhsT=w3_codes[:].bitcast(FP8X4), lhsT_scale=w3_scales[:],
                 rhs=hid_codes[:].bitcast(FP8X4), rhs_scale=hid_scales[:], start=True, stop=True,
             )
-            res = tile("res%d" % h, [P, HALF], F32)
-            nc.scalar.copy(res[:], acc[:])
-            nc.sync.dma_start(out[:, cols(h)], res[:])
+            res = tile("res%d" % n, [P, width], F32)
+            engines[emptier](res[:], acc[:, :width])
+            nc.sync.dma_start(out[:, h * HALF + c0 : h * HALF + c0 + width], res[:])

from contextlib import ExitStack

import concourse.mybir as mybir
from concourse.masks import make_identity

K, T, S, N, H, U = 512, 2048, 512, 128, 512, 1024
FLOPS = 2 * K * H * S * 2 + 2 * H * N * U

F32 = mybir.dt.float32
BF16 = mybir.dt.bfloat16
I32 = mybir.dt.int32
U32 = mybir.dt.uint32
U16 = mybir.dt.uint16
U8 = mybir.dt.uint8
FP8X4 = mybir.dt.float8_e4m3fn_x4
ALU = mybir.AluOpType
ACT = mybir.ActivationFunctionType

P = 128
PACK = 4
HALF = 512
HALVES = U // HALF
SPARE = 16
EPISTASIS = 0.7


def tile_picked_ymetmu_mh_p_kernel(
    tc, x_words, x_scales, w1, w2, g0, cap, unit, w3, offs, m1, m2, out
):
    nc = tc.nc
    with ExitStack() as ctx:
        keep = ctx.enter_context(tc.tile_pool(name="keep", bufs=1))
        ring = ctx.enter_context(tc.tile_pool(name="ring", bufs=5))
        psum = ctx.enter_context(tc.psum_pool(name="psum", bufs=1))

        def tile(name, shape, dtype):
            return keep.tile(shape, dtype, name=name, align_bytes=64)

        def bank(b):
            return psum.tile([P, HALF], F32, name="bank%d" % b)

        def load_list(name, src):
            lst = tile(name, src.shape, U16)
            nc.sync.dma_start(lst[:], src)
            return lst

        def load_weight(name, w):
            parts = []
            for c in range(2):
                raw = tile(name + "_raw%d" % c, [P, PACK, H // 2], F32)
                nc.sync.dma_start(raw[:], w.rearrange("(p j) c -> p j c", j=PACK)[:, :, c * (H // 2) : (c + 1) * (H // 2)])
                parts.append(raw)
            return parts

        def load_rows(name, src):
            tiles = []
            for t in range(PACK):
                rows = tile(name + "%d" % t, [P, U], F32)
                nc.sync.dma_start(rows[:], src.rearrange("(p t) r -> p t r", t=PACK)[:, t, :])
                tiles.append(rows)
            return tiles

        all_scales = tile("all_scales", [P, T], U8)
        nc.vector.memset(all_scales[:].bitcast(I32), 0)

        offs_sb = load_list("offs_sb", offs)
        for q in range(4):
            nc.sync.dma_start(
                all_scales[32 * q : 32 * q + 4, :].bitcast(I32),
                x_scales[0, 4 * q : 4 * q + 4, :].bitcast(I32),
            )
        all_words = tile("all_words", [P, T], I32)
        nc.sync.dma_start(all_words[:], x_words[0].rearrange("p c r -> p (c r)").bitcast(I32))
        w2_raw = load_weight("w2", w2)
        m1_sb = load_list("m1_sb", m1)
        m2_sb = load_list("m2_sb", m2)
        w1_raw = load_weight("w1", w1)
        g0_sb = load_rows("g0_", g0)
        w3_raw = tile("w3_raw", [P, PACK, N], F32)
        nc.sync.dma_start(w3_raw[:], w3.rearrange("(p j) n -> p j n", j=PACK))
        unit_sb = tile("unit_sb", [P, PACK], F32)
        nc.sync.dma_start(unit_sb[:], unit.rearrange("(p t) o -> p (t o)", t=PACK))
        cap_sb = load_rows("cap_", cap)

        ident = tile("ident", [P, P], F32)
        make_identity(nc, ident[:])

        def window(name):
            win = tile(name, [P, S + SPARE], F32)
            nc.gpsimd.memset(win[:, S:], 0.0)
            return win

        ep_win = [window("ep_win%d" % t) for t in range(PACK)]
        y_win = [window("y_win%d" % t) for t in range(PACK)]

        def deal(name, raw_parts, copies):
            dealt = tile(name + "_dealt", [P, PACK, P, PACK], BF16)
            for c, raw in enumerate(raw_parts):
                copies[c](
                    dealt[:, :, c * (P // 2) : (c + 1) * (P // 2), :].rearrange("p t m j -> p m t j"),
                    raw[:].rearrange("p j (m t) -> p m t j", t=PACK),
                )
            return dealt

        def quantize(name, values, width):
            codes = tile(name + "_codes", [P, width], U32)
            scales = tile(name + "_scales", [P, width], U8)
            nc.vector.quantize_mx(codes[:].bitcast(FP8X4), scales[:], values)
            return codes, scales

        def stationary(name, dealt, groups):
            res = []
            for t0, t1 in groups:
                codes, scales = quantize(name + "_%d" % t0, dealt[:, t0:t1].rearrange("p t m j -> p (t m j)"), (t1 - t0) * P)
                res.extend((codes[:, k * P : (k + 1) * P], scales[:, k * P : (k + 1) * P]) for k in range(t1 - t0))
            return res

        x_sc = tile("x_sc", [P, S], U8)
        nc.vector.tensor_copy(x_sc[:], all_scales[:].indirect(offs_sb[:]))
        x_wd = tile("x_wd", [P, S], I32)
        nc.vector.tensor_copy(x_wd[:].bitcast(U32), all_words[:].bitcast(U32).indirect(offs_sb[:]))

        def table(weights, b):
            codes, scales = weights
            acc = bank(b)
            nc.tensor.matmul_mx(
                acc[:], lhsT=codes.bitcast(FP8X4), lhsT_scale=scales,
                rhs=x_wd[:].bitcast(FP8X4), rhs_scale=x_sc[:], start=True, stop=True,
            )
            return acc

        w2_dealt = deal("w2", w2_raw, (nc.scalar.copy, nc.vector.tensor_copy))
        ep_acc = [table(w, 2 * t) for t, w in enumerate(stationary("w2", w2_dealt, ((0, 1), (1, 4))))]
        w1_dealt = deal("w1", w1_raw, (nc.vector.tensor_copy, nc.vector.tensor_copy))
        y_acc = [table(w, 2 * t + 1) for t, w in enumerate(stationary("w1", w1_dealt, ((0, 1), (1, 4))))]

        def picks(lst, h):
            return lst[:, h * (HALF // 16) : (h + 1) * (HALF // 16)]

        def cols(h):
            return slice(h * HALF, (h + 1) * HALF)

        def turned_sum(acc, terms):
            for b in range(HALF // P):
                blk = slice(b * P, (b + 1) * P)
                for k, term in enumerate(terms):
                    nc.tensor.matmul(
                        acc[:, blk], term[:, blk], ident[:], start=(k == 0), stop=(k == len(terms) - 1), is_transpose=True
                    )

        e1, epi, a2, part, nd, ratio, arg = {}, {}, {}, {}, {}, {}, {}
        fused = ()

        def first_factors(t):
            (nc.vector.tensor_copy if t in (2,) else nc.scalar.copy)(ep_win[t][:, :S], ep_acc[t][:])
            for h in range(HALVES):
                e1[t, h] = ring.tile([P, HALF], F32, name="e1")
                nc.scalar.activation(e1[t, h][:], ep_win[t][:].indirect(picks(m1_sb, h)), ACT.Copy, scale=-EPISTASIS)

        def products(t):
            if t in ():
                nc.vector.tensor_scalar(y_win[t][:, :S], y_acc[t][:], -1.0, None, ALU.mult)
            else:
                nc.scalar.activation(y_win[t][:, :S], y_acc[t][:], ACT.Copy, scale=-1.0)
            for h in range(HALVES):
                epi[t, h] = ring.tile([P, HALF], F32, name="epi")
                nc.vector.tensor_tensor(epi[t, h][:], ep_win[t][:].indirect(picks(m2_sb, h)), e1[t, h][:], ALU.mult)

        def sums(t):
            for h in range(HALVES):
                if (t, h) not in fused:
                    a2[t, h] = ring.tile([P, HALF], F32, name="a2")
                    nc.scalar.activation(a2[t, h][:], y_win[t][:].indirect(picks(m2_sb, h)), ACT.Copy)
            for h in range(HALVES):
                part[t, h] = ring.tile([P, HALF], F32, name="part")
                nc.vector.tensor_tensor(part[t, h][:], y_win[t][:].indirect(picks(m1_sb, h)), epi[t, h][:], ALU.add)
            for h in range(HALVES):
                nd[t, h] = tile("nd%d_%d" % (t, h), [P, HALF], F32)
                if (t, h) in fused:
                    nc.vector.tensor_tensor(nd[t, h][:], y_win[t][:].indirect(picks(m2_sb, h)), part[t, h][:], ALU.add)
                else:
                    nc.vector.tensor_tensor(nd[t, h][:], part[t, h][:], a2[t, h][:], ALU.add)

        def ratios(t):
            for h in range(HALVES):
                ratio[t, h] = tile("ratio%d_%d" % (t, h), [P, HALF], F32)
                nc.scalar.activation(ratio[t, h][:], nd[t, h][:], ACT.Exp)
                arg[t, h] = bank(2 * t + h)
                turned_sum(arg[t, h], [g0_sb[t][:, cols(h)], nd[t, h][:]])

        first_factors(0)
        for t in range(PACK):
            products(t)
            if t + 1 < PACK:
                first_factors(t + 1)
            if t > 0:
                ratios(t - 1)
            sums(t)
        ratios(PACK - 1)

        w3_dealt = tile("w3_dealt", [P, N, PACK], BF16)
        nc.vector.tensor_copy(w3_dealt[:], w3_raw[:].rearrange("p j n -> p n j"))
        w3_codes, w3_scales = quantize("w3", w3_dealt[:].rearrange("p n j -> p (n j)"), N)

        last = (PACK - 1, HALVES - 1)
        acr = {}
        room = [tile("acr%d" % k, [P, HALF], F32) for k in range(0)] + [epi[last], epi[PACK - 1, 0]]
        for u, (t, h) in enumerate((t, h) for t in range(PACK) for h in range(HALVES)):
            acr[t, h] = room[u]
            if u >= 0:
                room.append(ratio[t, h])
            nc.vector.tensor_tensor(acr[t, h][:], ratio[t, h][:], cap_sb[t][:, cols(h)], ALU.min)

        spent = [a2[last], part[last], nd[last]]
        hid = [tile("hid%d" % h, [P, PACK, HALF], BF16) for h in range(HALVES)]
        for u, (t, h) in enumerate((t, h) for h in range(HALVES) for t in range(PACK)):
            turned = spent[u % len(spent)]
            nc.scalar.activation(turned[:], arg[t, h][:], ACT.Sigmoid)
            fold = bank(2 * t + h)
            turned_sum(fold, [turned[:]])
            nc.vector.scalar_tensor_tensor(
                hid[h][:, t, :], fold[:], unit_sb[:, t : t + 1], acr[t, h][:], ALU.mult, ALU.mult
            )

        def gpsimd_copy(dst, src):
            nc.gpsimd.tensor_scalar(dst, src, 1.0, 0.0, ALU.mult, ALU.add)

        engines = {"s": nc.scalar.copy, "v": nc.vector.tensor_copy, "g": gpsimd_copy}
        pieces = [(0, 0, 256, (("s", 256),), "s"), (0, 256, 256, (("s", 256),), "s"), (1, 0, 256, (("v", 256),), "v"), (1, 256, 256, (("s", 256),), "s")]
        for n, (h, c0, width, shares, emptier) in enumerate(pieces):
            woven = tile("woven%d" % n, [P, width, PACK], BF16)
            at = 0
            for engine, share in shares:
                engines[engine](
                    woven[:, at : at + share, :].rearrange("p (c i) t -> p c t i", i=4),
                    hid[h][:, :, c0 + at : c0 + at + share].rearrange("p t (c i) -> p c t i", i=4),
                )
                at = at + share
            hid_codes, hid_scales = quantize("hid%d" % n, woven[:].rearrange("p c t -> p (c t)"), width)
            acc = bank((0, 2, 4, 6, 1)[n])
            nc.tensor.matmul_mx(
                acc[:, :width], lhsT=w3_codes[:].bitcast(FP8X4), lhsT_scale=w3_scales[:],
                rhs=hid_codes[:].bitcast(FP8X4), rhs_scale=hid_scales[:], start=True, stop=True,
            )
            res = tile("res%d" % n, [P, width], F32)
            engines[emptier](res[:], acc[:, :width])
            nc.sync.dma_start(out[:, h * HALF + c0 : h * HALF + c0 + width], res[:])
